import numpy as np
import ml_dtypes


def mxq(x, axis, fmt="e4m3"):
    dtype, down = {"e4m3": (ml_dtypes.float8_e4m3fn, 7), "e5m2": (ml_dtypes.float8_e5m2, 14)}[fmt]
    v = np.moveaxis(np.asarray(x, np.float32).astype(ml_dtypes.bfloat16).astype(np.float64), axis, -1)
    blocks = v.reshape(v.shape[:-1] + (-1, 32))
    amax = np.abs(blocks).max(-1, keepdims=True)
    byte = np.maximum(np.where(amax > 0, np.frexp(amax)[1] - 1 + 127, 0) - down, 1)
    scale = np.exp2(byte - 127.0)
    codes = (blocks / scale).astype(np.float32).astype(dtype).astype(np.float64)
    return np.moveaxis((codes * scale).reshape(v.shape), -1, axis)


WIDE = False


def mx_kscale(k):
    if not WIDE:
        return np.ones(k)
    levels = np.array([10, -10, 5, -5, 0])
    if k % 512:
        return np.exp2(np.random.permutation(np.resize(levels, k // 32))).repeat(32)
    a = np.empty((k // 512, 16))
    for p in range(k // 512):
        a[p, :8] = np.random.permutation(np.resize(levels, 8))
        for g in range(8):
            far = levels[np.abs(levels - a[p, g]) >= 10]
            a[p, g + 8] = far[np.random.randint(len(far))]
    return np.exp2(a.ravel()).repeat(32)


def f64(x):
    return np.asarray(x).astype(np.float64)


def striped(idx):
    return np.tile(idx.reshape(-1, 16).T, (8, 1)).astype(np.uint16)


def unstriped(offs):
    return offs[:16].T.reshape(-1).astype(np.int64)


E2M1 = np.array([0.0, 0.5, 1.0, 1.5, 2.0, 3.0, 4.0, 6.0, -0.0, -0.5, -1.0, -1.5, -2.0, -3.0, -4.0, -6.0])


def pack_weight(w, fmt):
    k, n = w.shape
    w = f64(np.asarray(w, np.float32).astype(ml_dtypes.bfloat16)).reshape(k // 32, 32, n)
    amax = np.abs(w).max(1)
    if fmt == "e4m3":
        byte = np.frexp(amax)[1] - 1 + 127 - 7
    else:
        mant, ex = np.frexp(amax / 6.0)
        byte = np.where(mant > 0.5, ex, ex - 1) + 127
    byte = np.clip(np.where(amax > 0, byte, 1), 1, 254)
    scaled = (w * np.exp2(127.0 - byte)[:, None, :]).reshape(k, n).astype(np.float32)
    by_word = np.ascontiguousarray(scaled.reshape(k // 512, 128, 4, n).transpose(0, 1, 3, 2))
    if fmt == "e4m3":
        words = by_word.astype(ml_dtypes.float8_e4m3fn).view(np.uint8)
    else:
        c = by_word.astype(ml_dtypes.float4_e2m1fn).view(np.uint8) & 0xF
        words = (c[..., 0::2] | (c[..., 1::2] << 4)).reshape(k // 512, 128, 2 * n)
    return np.ascontiguousarray(words), np.ascontiguousarray(byte.astype(np.uint8).reshape(k // 512, 16, n))


def unpack_weight(words, scales, fmt):
    g, _, n = scales.shape
    words = np.ascontiguousarray(words).reshape(g, 128, n, -1)
    if fmt == "e4m3":
        vals = words.view(ml_dtypes.float8_e4m3fn).astype(np.float64)
    else:
        nib = np.empty((g, 128, n, 4), np.uint8)
        nib[..., 0::2] = words & 0xF
        nib[..., 1::2] = words >> 4
        vals = E2M1[nib]
    vals = vals * np.repeat(np.exp2(scales.astype(np.float64) - 127.0), 8, axis=1)[..., None]
    return vals.transpose(0, 1, 3, 2).reshape(g * 512, n)


def silu(v):
    return v / (1.0 + np.exp(-np.maximum(v, -700.0)))


K, M, T, S = 1024, 256, 4096, 1536


def setup_inputs():
    n = np.random.standard_normal
    s = mx_kscale(K)[:, None]
    v = pack_weight(n((K, T)) * s, "e4m3")
    p_w4 = pack_weight(n((K, M)) / np.sqrt(K) / s, "e2m1")
    return {
        "tab_words": v[0],
        "tab_scales": v[1],
        "w4_words": p_w4[0],
        "w4_scales": p_w4[1],
        "dw": (n((K, M)) / np.sqrt(K) / s).astype(np.float32),
        "rT": n((M, T)).astype(np.float32),
        "b": (0.3 * n(256)).astype(np.float32),
        "offs": striped(np.random.permutation(T)[:S]),
    }


def reference(tab_words, tab_scales, w4_words, w4_scales, dw, rT, b, offs):
    tab_ = unpack_weight(tab_words, tab_scales, "e4m3")[:, unstriped(offs)]
    w4_ = unpack_weight(w4_words, w4_scales, "e2m1")
    dw_ = mxq(f64(dw), 0, "e4m3")
    y = w4_.T @ tab_ + dw_.T @ tab_
    return (silu(y + f64(b)[:, None])) + f64(rT)[:, unstriped(offs)]

@@ -1,0 +1,160 @@
+from contextlib import ExitStack
+
+import concourse.mybir as mybir
+
+K, M, T, S = 1024, 256, 4096, 1536
+FLOPS = 2 * 2 * K * M * S
+
+F32 = mybir.dt.float32
+BF16 = mybir.dt.bfloat16
+I32 = mybir.dt.int32
+U32 = mybir.dt.uint32
+U16 = mybir.dt.uint16
+U8 = mybir.dt.uint8
+FP8X4 = mybir.dt.float8_e4m3fn_x4
+FP4X4 = mybir.dt.float4_e2m1fn_x4
+SILU = mybir.ActivationFunctionType.Silu
+ADD = mybir.AluOpType.add
+
+P = 128
+PACK = 4
+PASSES = K // (P * PACK)
+HALVES = M // P
+BANK = 512
+SLICES = S // BANK
+GROUP = 16
+QUADS = 4
+QUAD = P // QUADS
+ROWS = 4
+FIRST_ROW = P - PASSES * QUADS * ROWS
+PIECES = ((512, 512, 512), (512, 512, 256, 256))
+
+
+def tile_list_tabres_silu_kernel(
+    tc, tab_words, tab_scales, w4_words, w4_scales, dw, rT, b, offs, out
+):
+    nc = tc.nc
+    with ExitStack() as ctx:
+        lists = ctx.enter_context(tc.tile_pool(name="lists", bufs=1))
+        keep = ctx.enter_context(tc.tile_pool(name="keep", bufs=1))
+        psum = ctx.enter_context(tc.psum_pool(name="psum", bufs=1))
+
+        offsets = lists.tile([P, S // GROUP], U16, name="offsets")
+        nc.sync.dma_start(offsets[:], offs)
+
+        def picked(window, first, count):
+            return window.indirect(offsets[:, first // GROUP : (first + count) // GROUP])
+
+        scale_rows = keep.tile([P, T], U8, name="scale_rows", tag="window_a")
+        nc.sync.dma_start(
+            scale_rows[FIRST_ROW:P, :].bitcast(I32),
+            tab_scales.rearrange("a q t -> q a t").bitcast(I32),
+        )
+
+        words = []
+        words0 = keep.tile([P, T], U32, name="words0", tag="window_b")
+        nc.sync.dma_start(words0[:].bitcast(I32), tab_words[0].rearrange("p t i -> p (t i)").bitcast(I32))
+        words.append(words0)
+
+        w4_codes = keep.tile([P, PASSES, 2 * M], U8, name="w4_codes", align_bytes=64)
+        nc.sync.dma_start(w4_codes[:].bitcast(I32), w4_words.rearrange("a p c -> p a c").bitcast(I32))
+
+        dw_raw = []
+        for a in range(PASSES):
+            raw = keep.tile([P, PACK, M], F32, name=f"dw_raw{a}")
+            nc.sync.dma_start(raw[:], dw[a * P * PACK : (a + 1) * P * PACK, :].rearrange("(p i) n -> p i n", i=PACK))
+            dw_raw.append(raw)
+
+        words1 = keep.tile([P, T], U32, name="words1")
+        nc.sync.dma_start(words1[:].bitcast(I32), tab_words[1].rearrange("p t i -> p (t i)").bitcast(I32))
+        words.append(words1)
+
+        w4_plane = keep.tile([P, PASSES * M], U8, name="w4_plane", align_bytes=64)
+        nc.vector.memset(w4_plane[:].bitcast(I32), 0)
+        nc.vector.memset(scale_rows[0:FIRST_ROW, :].bitcast(I32), 0)
+        for q in range(QUADS):
+            nc.gpsimd.dma_start(
+                w4_plane[QUAD * q : QUAD * q + ROWS, :].bitcast(I32).rearrange("r (a n) -> r a n", a=PASSES),
+                w4_scales[:, ROWS * q : ROWS * (q + 1), :].rearrange("a r n -> r a n").bitcast(I32),
+            )
+        bias = keep.tile([P, HALVES], F32, name="bias")
+        with nc.allow_non_contiguous_dma(reason="one bias value a partition"):
+            nc.scalar.dma_start(bias[:], b.rearrange("(h p) -> p h", p=P))
+
+        tab_plane = keep.tile([P, PASSES * S], U8, name="tab_plane", align_bytes=64)
+        nc.vector.memset(tab_plane[:].bitcast(I32), 0)
+
+        picked_scales = keep.tile([P, S], U8, name="picked_scales")
+        nc.vector.tensor_copy(picked_scales[:], picked(scale_rows[:], 0, S))
+        for q in range(QUADS):
+            nc.scalar.dma_start(
+                tab_plane[QUAD * q : QUAD * q + ROWS, :].bitcast(I32).rearrange("r (a j) -> r a j", a=PASSES),
+                picked_scales[FIRST_ROW + PASSES * ROWS * q : FIRST_ROW + PASSES * ROWS * (q + 1), :].bitcast(I32),
+            )
+
+        codes = [keep.tile([P, S], U32, name=f"codes{a}", align_bytes=64) for a in range(PASSES)]
+        nc.vector.tensor_copy(codes[0][:], picked(words[0][:], 0, S))
+
+        residual = []
+        for h, tag in enumerate(("window_a", "window_b")):
+            rows = keep.tile([P, T], F32, name=f"residual{h}", tag=tag)
+            nc.sync.dma_start(rows[:], rT[h * P : (h + 1) * P, :])
+            residual.append(rows)
+
+        dw_codes, dw_plane = [], []
+        for a in range(PASSES):
+            grouped = keep.tile([P, M, PACK], BF16, name=f"dw_grouped{a}", align_bytes=64)
+            nc.scalar.copy(
+                grouped[:].rearrange("p (c n) i -> p c i n", n=4),
+                dw_raw[a][:].rearrange("p i (c n) -> p c i n", n=4),
+            )
+            dcodes = keep.tile([P, M], U32, name=f"dw_codes{a}", align_bytes=64)
+            dplane = keep.tile([P, M], U8, name=f"dw_plane{a}", align_bytes=64)
+            nc.vector.quantize_mx(dcodes[:].bitcast(FP8X4), dplane[:], grouped[:].rearrange("p n i -> p (n i)"))
+            dw_codes.append(dcodes)
+            dw_plane.append(dplane)
+
+        banks = [[psum.tile([P, BANK], F32, name=f"y{h}_{s}") for s in range(SLICES)] for h in range(HALVES)]
+
+        def multiply(a, h, s):
+            cols = slice(s * BANK, (s + 1) * BANK)
+            rhs = codes[a][:, cols].bitcast(FP8X4)
+            rhs_scale = tab_plane[:, a * S + s * BANK : a * S + (s + 1) * BANK]
+            nc.tensor.matmul_mx(
+                banks[h][s][:],
+                lhsT=w4_codes[:, a, 2 * h * P : 2 * (h + 1) * P].bitcast(FP4X4),
+                lhsT_scale=w4_plane[:, a * M + h * P : a * M + (h + 1) * P],
+                rhs=rhs,
+                rhs_scale=rhs_scale,
+                start=(a == 0),
+                stop=False,
+            )
+            nc.tensor.matmul_mx(
+                banks[h][s][:],
+                lhsT=dw_codes[a][:, h * P : (h + 1) * P].bitcast(FP8X4),
+                lhsT_scale=dw_plane[a][:, h * P : (h + 1) * P],
+                rhs=rhs,
+                rhs_scale=rhs_scale,
+                start=False,
+                stop=(a == PASSES - 1),
+            )
+
+        for h in range(HALVES):
+            for s in range(SLICES):
+                multiply(0, h, s)
+        for s in range(SLICES):
+            nc.vector.tensor_copy(codes[1][:, s * BANK : (s + 1) * BANK], picked(words[1][:], s * BANK, BANK))
+
+        for h in range(HALVES):
+            act = keep.tile([P, S], F32, name=f"act{h}")
+            for s in range(SLICES):
+                multiply(1, h, s)
+                nc.scalar.activation(act[:, s * BANK : (s + 1) * BANK], banks[h][s][:], SILU, bias=bias[:, h : h + 1])
+            first = 0
+            for i, count in enumerate(PIECES[h]):
+                result = keep.tile([P, count], F32, name=f"result{h}_{i}")
+                nc.vector.tensor_tensor(
+                    result[:], picked(residual[h][:], first, count), act[:, first : first + count], ADD
+                )
+                nc.sync.dma_start(out[h * P : (h + 1) * P, first : first + count], result[:])
+                first = first + count

@@ -27,7 +27,8 @@ QUADS = 4
 QUAD = P // QUADS
 ROWS = 4
 FIRST_ROW = P - PASSES * QUADS * ROWS
-PIECES = ((512, 512, 512), (512, 512, 256, 256))
+STAGED = S + M
+PIECES = ((512, 512, 512), (512, 512, 384, 128))
 
 
 def tile_list_tabres_silu_kernel(
@@ -45,10 +46,16 @@ def tile_list_tabres_silu_kernel(
         def picked(window, first, count):
             return window.indirect(offsets[:, first // GROUP : (first + count) // GROUP])
 
-        scale_rows = keep.tile([P, T], U8, name="scale_rows", tag="window_a")
+        scale_rows = keep.tile([P, T], U8, name="scale_rows")
         nc.sync.dma_start(
             scale_rows[FIRST_ROW:P, :].bitcast(I32),
             tab_scales.rearrange("a q t -> q a t").bitcast(I32),
+        )
+
+        staged = keep.tile([P, STAGED], U8, name="staged")
+        nc.sync.dma_start(
+            staged[FIRST_ROW:P, S:STAGED].bitcast(I32),
+            w4_scales.rearrange("a q n -> q a n").bitcast(I32),
         )
 
         words = []
@@ -59,55 +66,51 @@ def tile_list_tabres_silu_kernel(
         w4_codes = keep.tile([P, PASSES, 2 * M], U8, name="w4_codes", align_bytes=64)
         nc.sync.dma_start(w4_codes[:].bitcast(I32), w4_words.rearrange("a p c -> p a c").bitcast(I32))
 
-        dw_raw = []
-        for a in range(PASSES):
-            raw = keep.tile([P, PACK, M], F32, name=f"dw_raw{a}")
-            nc.sync.dma_start(raw[:], dw[a * P * PACK : (a + 1) * P * PACK, :].rearrange("(p i) n -> p i n", i=PACK))
-            dw_raw.append(raw)
+        dw_raw = keep.tile([P, PASSES, PACK * M], F32, name="dw_raw", tag="window_c")
+        nc.sync.dma_start(dw_raw[:], dw.rearrange("(a p i) n -> p a (i n)", a=PASSES, i=PACK))
 
-        words1 = keep.tile([P, T], U32, name="words1")
-        nc.sync.dma_start(words1[:].bitcast(I32), tab_words[1].rearrange("p t i -> p (t i)").bitcast(I32))
-        words.append(words1)
-
-        w4_plane = keep.tile([P, PASSES * M], U8, name="w4_plane", align_bytes=64)
-        nc.vector.memset(w4_plane[:].bitcast(I32), 0)
         nc.vector.memset(scale_rows[0:FIRST_ROW, :].bitcast(I32), 0)
-        for q in range(QUADS):
-            nc.gpsimd.dma_start(
-                w4_plane[QUAD * q : QUAD * q + ROWS, :].bitcast(I32).rearrange("r (a n) -> r a n", a=PASSES),
-                w4_scales[:, ROWS * q : ROWS * (q + 1), :].rearrange("a r n -> r a n").bitcast(I32),
-            )
         bias = keep.tile([P, HALVES], F32, name="bias")
         with nc.allow_non_contiguous_dma(reason="one bias value a partition"):
             nc.scalar.dma_start(bias[:], b.rearrange("(h p) -> p h", p=P))
 
-        tab_plane = keep.tile([P, PASSES * S], U8, name="tab_plane", align_bytes=64)
-        nc.vector.memset(tab_plane[:].bitcast(I32), 0)
+        planes = keep.tile([P, PASSES * STAGED], U8, name="planes", align_bytes=64)
+        nc.vector.memset(planes[:].bitcast(I32), 0)
 
-        picked_scales = keep.tile([P, S], U8, name="picked_scales")
+        picked_scales = keep.tile([P, S], U8, name="picked_scales", tag="window_a")
         nc.vector.tensor_copy(picked_scales[:], picked(scale_rows[:], 0, S))
-        for q in range(QUADS):
-            nc.scalar.dma_start(
-                tab_plane[QUAD * q : QUAD * q + ROWS, :].bitcast(I32).rearrange("r (a j) -> r a j", a=PASSES),
-                picked_scales[FIRST_ROW + PASSES * ROWS * q : FIRST_ROW + PASSES * ROWS * (q + 1), :].bitcast(I32),
+        nc.vector.tensor_copy(staged[FIRST_ROW:P, 0:S].bitcast(I32), picked_scales[FIRST_ROW:P, :].bitcast(I32))
+        for q in (0, 2, 1, 3):
+            nc.sync.dma_start(
+                planes[QUAD * q : QUAD * q + ROWS, :].bitcast(I32).rearrange("r (a j) -> r a j", a=PASSES),
+                staged[FIRST_ROW + PASSES * ROWS * q : FIRST_ROW + PASSES * ROWS * (q + 1), :].bitcast(I32),
             )
+
+        words1 = keep.tile([P, T], U32, name="words1", tag="window_a")
+        nc.sync.dma_start(words1[:].bitcast(I32), tab_words[1].rearrange("p t i -> p (t i)").bitcast(I32))
+        words.append(words1)
 
         codes = [keep.tile([P, S], U32, name=f"codes{a}", align_bytes=64) for a in range(PASSES)]
         nc.vector.tensor_copy(codes[0][:], picked(words[0][:], 0, S))
 
+        dw_grouped = []
+        for a in range(PASSES):
+            grouped = keep.tile([P, M, PACK], BF16, name=f"dw_grouped{a}", align_bytes=64)
+            nc.vector.tensor_copy(
+                grouped[:].rearrange("p (c n) i -> p c i n", n=4),
+                dw_raw[:, a, :].rearrange("p (i c n) -> p c i n", i=PACK, n=4),
+            )
+            dw_grouped.append(grouped)
+
         residual = []
-        for h, tag in enumerate(("window_a", "window_b")):
+        for h, tag in enumerate(("window_b", "window_c")):
             rows = keep.tile([P, T], F32, name=f"residual{h}", tag=tag)
             nc.sync.dma_start(rows[:], rT[h * P : (h + 1) * P, :])
             residual.append(rows)
 
         dw_codes, dw_plane = [], []
         for a in range(PASSES):
-            grouped = keep.tile([P, M, PACK], BF16, name=f"dw_grouped{a}", align_bytes=64)
-            nc.scalar.copy(
-                grouped[:].rearrange("p (c n) i -> p c i n", n=4),
-                dw_raw[a][:].rearrange("p i (c n) -> p c i n", n=4),
-            )
+            grouped = dw_grouped[a]
             dcodes = keep.tile([P, M], U32, name=f"dw_codes{a}", align_bytes=64)
             dplane = keep.tile([P, M], U8, name=f"dw_plane{a}", align_bytes=64)
             nc.vector.quantize_mx(dcodes[:].bitcast(FP8X4), dplane[:], grouped[:].rearrange("p n i -> p (n i)"))
@@ -116,39 +119,40 @@ def tile_list_tabres_silu_kernel(
 
         banks = [[psum.tile([P, BANK], F32, name=f"y{h}_{s}") for s in range(SLICES)] for h in range(HALVES)]
 
-        def multiply(a, h, s):
-            cols = slice(s * BANK, (s + 1) * BANK)
-            rhs = codes[a][:, cols].bitcast(FP8X4)
-            rhs_scale = tab_plane[:, a * S + s * BANK : a * S + (s + 1) * BANK]
+        def multiply(a, h, s, lhsT, lhsT_scale, start=False, stop=False):
             nc.tensor.matmul_mx(
                 banks[h][s][:],
-                lhsT=w4_codes[:, a, 2 * h * P : 2 * (h + 1) * P].bitcast(FP4X4),
-                lhsT_scale=w4_plane[:, a * M + h * P : a * M + (h + 1) * P],
-                rhs=rhs,
-                rhs_scale=rhs_scale,
-                start=(a == 0),
-                stop=False,
+                lhsT=lhsT,
+                lhsT_scale=lhsT_scale,
+                rhs=codes[a][:, s * BANK : (s + 1) * BANK].bitcast(FP8X4),
+                rhs_scale=planes[:, a * STAGED + s * BANK : a * STAGED + (s + 1) * BANK],
+                start=start,
+                stop=stop,
             )
-            nc.tensor.matmul_mx(
-                banks[h][s][:],
-                lhsT=dw_codes[a][:, h * P : (h + 1) * P].bitcast(FP8X4),
-                lhsT_scale=dw_plane[a][:, h * P : (h + 1) * P],
-                rhs=rhs,
-                rhs_scale=rhs_scale,
-                start=False,
-                stop=(a == PASSES - 1),
+
+        def w4_operand(a, h):
+            return (
+                w4_codes[:, a, 2 * h * P : 2 * (h + 1) * P].bitcast(FP4X4),
+                planes[:, a * STAGED + S + h * P : a * STAGED + S + (h + 1) * P],
             )
+
+        def dw_operand(a, h):
+            return dw_codes[a][:, h * P : (h + 1) * P].bitcast(FP8X4), dw_plane[a][:, h * P : (h + 1) * P]
 
         for h in range(HALVES):
             for s in range(SLICES):
-                multiply(0, h, s)
+                multiply(0, h, s, *w4_operand(0, h), start=True)
+        for h in range(HALVES):
+            for s in range(SLICES):
+                multiply(0, h, s, *dw_operand(0, h))
         for s in range(SLICES):
             nc.vector.tensor_copy(codes[1][:, s * BANK : (s + 1) * BANK], picked(words[1][:], s * BANK, BANK))
 
         for h in range(HALVES):
             act = keep.tile([P, S], F32, name=f"act{h}")
             for s in range(SLICES):
-                multiply(1, h, s)
+                multiply(1, h, s, *w4_operand(1, h))
+                multiply(1, h, s, *dw_operand(1, h), stop=True)
                 nc.scalar.activation(act[:, s * BANK : (s + 1) * BANK], banks[h][s][:], SILU, bias=bias[:, h : h + 1])
             first = 0
             for i, count in enumerate(PIECES[h]):

@@ -28,6 +28,7 @@ QUAD = P // QUADS
 ROWS = 4
 FIRST_ROW = P - PASSES * QUADS * ROWS
 STAGED = S + M
+BIAS_STEP = QUAD // HALVES
 PIECES = ((512, 512, 512), (512, 512, 384, 128))
 
 
@@ -69,10 +70,10 @@ def tile_list_tabres_silu_kernel(
         dw_raw = keep.tile([P, PASSES, PACK * M], F32, name="dw_raw", tag="window_c")
         nc.sync.dma_start(dw_raw[:], dw.rearrange("(a p i) n -> p a (i n)", a=PASSES, i=PACK))
 
+        bias_rows = keep.tile([P, QUAD], F32, name="bias_rows", align_bytes=64)
+        nc.vector.memset(bias_rows[:], 0.0)
+        nc.scalar.dma_start(bias_rows[0:P:BIAS_STEP, :], b.rearrange("(h q c) -> q h c", h=HALVES, q=QUADS))
         nc.vector.memset(scale_rows[0:FIRST_ROW, :].bitcast(I32), 0)
-        bias = keep.tile([P, HALVES], F32, name="bias")
-        with nc.allow_non_contiguous_dma(reason="one bias value a partition"):
-            nc.scalar.dma_start(bias[:], b.rearrange("(h p) -> p h", p=P))
 
         planes = keep.tile([P, PASSES * STAGED], U8, name="planes", align_bytes=64)
         nc.vector.memset(planes[:].bitcast(I32), 0)
@@ -92,6 +93,9 @@ def tile_list_tabres_silu_kernel(
 
         codes = [keep.tile([P, S], U32, name=f"codes{a}", align_bytes=64) for a in range(PASSES)]
         nc.vector.tensor_copy(codes[0][:], picked(words[0][:], 0, S))
+
+        bias = keep.tile([P, QUAD], F32, name="bias", align_bytes=64)
+        nc.vector.transpose(bias[:], bias_rows[:])
 
         dw_grouped = []
         for a in range(PASSES):
@@ -153,7 +157,7 @@ def tile_list_tabres_silu_kernel(
             for s in range(SLICES):
                 multiply(1, h, s, *w4_operand(1, h))
                 multiply(1, h, s, *dw_operand(1, h), stop=True)
-                nc.scalar.activation(act[:, s * BANK : (s + 1) * BANK], banks[h][s][:], SILU, bias=bias[:, h : h + 1])
+                nc.scalar.activation(act[:, s * BANK : (s + 1) * BANK], banks[h][s][:], SILU, bias=bias[:, h * BIAS_STEP : h * BIAS_STEP + 1])
             first = 0
             for i, count in enumerate(PIECES[h]):
                 result = keep.tile([P, count], F32, name=f"result{h}_{i}")

from contextlib import ExitStack

import concourse.mybir as mybir

K, M, T, S = 1024, 256, 4096, 1536
FLOPS = 2 * 2 * K * M * S

F32 = mybir.dt.float32
BF16 = mybir.dt.bfloat16
I32 = mybir.dt.int32
U32 = mybir.dt.uint32
U16 = mybir.dt.uint16
U8 = mybir.dt.uint8
FP8X4 = mybir.dt.float8_e4m3fn_x4
FP4X4 = mybir.dt.float4_e2m1fn_x4
SILU = mybir.ActivationFunctionType.Silu
ADD = mybir.AluOpType.add

P = 128
PACK = 4
PASSES = K // (P * PACK)
HALVES = M // P
BANK = 512
SLICES = S // BANK
GROUP = 16
QUADS = 4
QUAD = P // QUADS
ROWS = 4
FIRST_ROW = P - PASSES * QUADS * ROWS
STAGED = S + M
BIAS_STEP = QUAD // HALVES
PIECES = ((512, 512, 512), (512, 512, 384, 128))


def tile_list_tabres_silu_kernel(
    tc, tab_words, tab_scales, w4_words, w4_scales, dw, rT, b, offs, out
):
    nc = tc.nc
    with ExitStack() as ctx:
        lists = ctx.enter_context(tc.tile_pool(name="lists", bufs=1))
        keep = ctx.enter_context(tc.tile_pool(name="keep", bufs=1))
        psum = ctx.enter_context(tc.psum_pool(name="psum", bufs=1))

        offsets = lists.tile([P, S // GROUP], U16, name="offsets")
        nc.sync.dma_start(offsets[:], offs)

        def picked(window, first, count):
            return window.indirect(offsets[:, first // GROUP : (first + count) // GROUP])

        scale_rows = keep.tile([P, T], U8, name="scale_rows")
        nc.sync.dma_start(
            scale_rows[FIRST_ROW:P, :].bitcast(I32),
            tab_scales.rearrange("a q t -> q a t").bitcast(I32),
        )

        staged = keep.tile([P, STAGED], U8, name="staged")
        nc.sync.dma_start(
            staged[FIRST_ROW:P, S:STAGED].bitcast(I32),
            w4_scales.rearrange("a q n -> q a n").bitcast(I32),
        )

        words = []
        words0 = keep.tile([P, T], U32, name="words0", tag="window_b")
        nc.sync.dma_start(words0[:].bitcast(I32), tab_words[0].rearrange("p t i -> p (t i)").bitcast(I32))
        words.append(words0)

        w4_codes = keep.tile([P, PASSES, 2 * M], U8, name="w4_codes", align_bytes=64)
        nc.sync.dma_start(w4_codes[:].bitcast(I32), w4_words.rearrange("a p c -> p a c").bitcast(I32))

        dw_raw = keep.tile([P, PASSES, PACK * M], F32, name="dw_raw", tag="window_c")
        nc.sync.dma_start(dw_raw[:], dw.rearrange("(a p i) n -> p a (i n)", a=PASSES, i=PACK))

        bias_rows = keep.tile([P, QUAD], F32, name="bias_rows", align_bytes=64)
        nc.vector.memset(bias_rows[:], 0.0)
        nc.scalar.dma_start(bias_rows[0:P:BIAS_STEP, :], b.rearrange("(h q c) -> q h c", h=HALVES, q=QUADS))
        nc.vector.memset(scale_rows[0:FIRST_ROW, :].bitcast(I32), 0)

        planes = keep.tile([P, PASSES * STAGED], U8, name="planes", align_bytes=64)
        nc.vector.memset(planes[:].bitcast(I32), 0)

        picked_scales = keep.tile([P, S], U8, name="picked_scales", tag="window_a")
        nc.vector.tensor_copy(picked_scales[:], picked(scale_rows[:], 0, S))
        nc.vector.tensor_copy(staged[FIRST_ROW:P, 0:S].bitcast(I32), picked_scales[FIRST_ROW:P, :].bitcast(I32))
        for q in (0, 2, 1, 3):
            nc.sync.dma_start(
                planes[QUAD * q : QUAD * q + ROWS, :].bitcast(I32).rearrange("r (a j) -> r a j", a=PASSES),
                staged[FIRST_ROW + PASSES * ROWS * q : FIRST_ROW + PASSES * ROWS * (q + 1), :].bitcast(I32),
            )

        words1 = keep.tile([P, T], U32, name="words1", tag="window_a")
        nc.sync.dma_start(words1[:].bitcast(I32), tab_words[1].rearrange("p t i -> p (t i)").bitcast(I32))
        words.append(words1)

        codes = [keep.tile([P, S], U32, name=f"codes{a}", align_bytes=64) for a in range(PASSES)]
        nc.vector.tensor_copy(codes[0][:], picked(words[0][:], 0, S))

        bias = keep.tile([P, QUAD], F32, name="bias", align_bytes=64)
        nc.vector.transpose(bias[:], bias_rows[:])

        dw_grouped = []
        for a in range(PASSES):
            grouped = keep.tile([P, M, PACK], BF16, name=f"dw_grouped{a}", align_bytes=64)
            nc.vector.tensor_copy(
                grouped[:].rearrange("p (c n) i -> p c i n", n=4),
                dw_raw[:, a, :].rearrange("p (i c n) -> p c i n", i=PACK, n=4),
            )
            dw_grouped.append(grouped)

        residual = []
        for h, tag in enumerate(("window_b", "window_c")):
            rows = keep.tile([P, T], F32, name=f"residual{h}", tag=tag)
            nc.sync.dma_start(rows[:], rT[h * P : (h + 1) * P, :])
            residual.append(rows)

        dw_codes, dw_plane = [], []
        for a in range(PASSES):
            grouped = dw_grouped[a]
            dcodes = keep.tile([P, M], U32, name=f"dw_codes{a}", align_bytes=64)
            dplane = keep.tile([P, M], U8, name=f"dw_plane{a}", align_bytes=64)
            nc.vector.quantize_mx(dcodes[:].bitcast(FP8X4), dplane[:], grouped[:].rearrange("p n i -> p (n i)"))
            dw_codes.append(dcodes)
            dw_plane.append(dplane)

        banks = [[psum.tile([P, BANK], F32, name=f"y{h}_{s}") for s in range(SLICES)] for h in range(HALVES)]

        def multiply(a, h, s, lhsT, lhsT_scale, start=False, stop=False):
            nc.tensor.matmul_mx(
                banks[h][s][:],
                lhsT=lhsT,
                lhsT_scale=lhsT_scale,
                rhs=codes[a][:, s * BANK : (s + 1) * BANK].bitcast(FP8X4),
                rhs_scale=planes[:, a * STAGED + s * BANK : a * STAGED + (s + 1) * BANK],
                start=start,
                stop=stop,
            )

        def w4_operand(a, h):
            return (
                w4_codes[:, a, 2 * h * P : 2 * (h + 1) * P].bitcast(FP4X4),
                planes[:, a * STAGED + S + h * P : a * STAGED + S + (h + 1) * P],
            )

        def dw_operand(a, h):
            return dw_codes[a][:, h * P : (h + 1) * P].bitcast(FP8X4), dw_plane[a][:, h * P : (h + 1) * P]

        for h in range(HALVES):
            for s in range(SLICES):
                multiply(0, h, s, *w4_operand(0, h), start=True)
        for h in range(HALVES):
            for s in range(SLICES):
                multiply(0, h, s, *dw_operand(0, h))
        for s in range(SLICES):
            nc.vector.tensor_copy(codes[1][:, s * BANK : (s + 1) * BANK], picked(words[1][:], s * BANK, BANK))

        for h in range(HALVES):
            act = keep.tile([P, S], F32, name=f"act{h}")
            for s in range(SLICES):
                multiply(1, h, s, *w4_operand(1, h))
                multiply(1, h, s, *dw_operand(1, h), stop=True)
                nc.scalar.activation(act[:, s * BANK : (s + 1) * BANK], banks[h][s][:], SILU, bias=bias[:, h * BIAS_STEP : h * BIAS_STEP + 1])
            first = 0
            for i, count in enumerate(PIECES[h]):
                result = keep.tile([P, count], F32, name=f"result{h}_{i}")
                nc.vector.tensor_tensor(
                    result[:], picked(residual[h][:], first, count), act[:, first : first + count], ADD
                )
                nc.sync.dma_start(out[h * P : (h + 1) * P, first : first + count], result[:])
                first = first + count
